import numpy as np
CORES = [5,6,7,13,14,15]
N = 6
GROUPS = [[0,1,2],[3,4,5]]
def setup_inputs(rng):
    return {"x": rng.standard_normal((N, 128, 1023), dtype=np.float32)}
def reference(x):
    y = np.empty((N, 128, 1023), x.dtype)
    for g in GROUPS:
        n = len(g); b = x.shape[2] // n
        for i, r in enumerate(g):
            y[r] = np.concatenate([x[s][:, i * b:(i + 1) * b] for s in g], axis=1)
    return {"y": y}

from concourse.bass import DstId, RemoteDMATransfer

MAX_GROUP = 3

SCRATCH = {
    "stage": ("sbuf", [128, 1023], "float32"),
    "land": ("sbuf", [128, 1023], "float32"),
}
SEMAPHORES = ["home", "loaded", "read", "stored"] + ["arr%d" % j for j in range(MAX_GROUP)]


def rank_program(g, core, T, topo):
    rank = T.rank_of(core)
    if rank is None:
        return

    group = [grp for grp in T.tables["GROUPS"] if rank in grp][0]
    n = len(group)
    i = group.index(rank)
    b = T.x.shape[1] // n
    peers = [j for j in range(n) if j != i]
    queues = [g.sync, g.scalar]

    def blk(j):
        return slice(j * b, (j + 1) * b)

    for k, j in enumerate(peers):
        queues[k % 2].dma_start(T.stage[:, blk(j)], T.x[:, blk(j)]).then_inc(T.sem.loaded, 16)

    g.dma_start(T.y[:, blk(i)], T.x[:, blk(i)]).then_inc(T.sem.home, 16)

    eng = 16
    while eng * len(peers) > 16:
        eng //= 2

    g.wait_ge(T.sem.loaded, 16 * len(peers))
    transfers = []
    for k, j in enumerate(peers):
        rid, pid, _se = topo.addr(T.cores[group[j]])
        transfers.append(RemoteDMATransfer(
            dst_ids=[DstId(rid=rid, pnc=pid)],
            dma_engine_mask=((1 << eng) - 1) << (k * eng),
            remote_sem=T.sem["arr%d" % i],
            src=T.stage[:, blk(j)],
            dst=T.land[:, blk(i)],
        ))
    g.remote_dma_fused(transfers, local_sem=T.sem.read)

    for k, j in enumerate(peers):
        q = queues[k % 2]
        q.wait_ge(T.sem["arr%d" % j], eng)
        q.dma_start(T.y[:, blk(j)], T.land[:, blk(j)]).then_inc(T.sem.stored, 16)

    g.wait_ge(T.sem.read, eng * len(peers))
    g.wait_ge(T.sem.home, 16)
    g.wait_ge(T.sem.stored, 16 * len(peers))
